import numpy as np
import ml_dtypes


def mxq(x, axis, fmt="e4m3"):
    dtype, down = {"e4m3": (ml_dtypes.float8_e4m3fn, 7), "e5m2": (ml_dtypes.float8_e5m2, 14)}[fmt]
    v = np.moveaxis(np.asarray(x, np.float32).astype(ml_dtypes.bfloat16).astype(np.float64), axis, -1)
    blocks = v.reshape(v.shape[:-1] + (-1, 32))
    amax = np.abs(blocks).max(-1, keepdims=True)
    byte = np.maximum(np.where(amax > 0, np.frexp(amax)[1] - 1 + 127, 0) - down, 1)
    scale = np.exp2(byte - 127.0)
    codes = (blocks / scale).astype(np.float32).astype(dtype).astype(np.float64)
    return np.moveaxis((codes * scale).reshape(v.shape), -1, axis)


WIDE = False


def mx_kscale(k):
    if not WIDE:
        return np.ones(k)
    levels = np.array([10, -10, 5, -5, 0])
    if k % 512:
        return np.exp2(np.random.permutation(np.resize(levels, k // 32))).repeat(32)
    a = np.empty((k // 512, 16))
    for p in range(k // 512):
        a[p, :8] = np.random.permutation(np.resize(levels, 8))
        for g in range(8):
            far = levels[np.abs(levels - a[p, g]) >= 10]
            a[p, g + 8] = far[np.random.randint(len(far))]
    return np.exp2(a.ravel()).repeat(32)


def f64(x):
    return np.asarray(x).astype(np.float64)


def striped(idx):
    return np.tile(np.asarray(idx).reshape(-1, 16).T, (8, 1)).astype(np.uint16)


def unstriped(offs):
    return offs[:16].T.reshape(-1).astype(np.int64)


E2M1 = np.array([0.0, 0.5, 1.0, 1.5, 2.0, 3.0, 4.0, 6.0, -0.0, -0.5, -1.0, -1.5, -2.0, -3.0, -4.0, -6.0])


def pack_weight(w, fmt):
    k, n = w.shape
    w = f64(np.asarray(w, np.float32).astype(ml_dtypes.bfloat16)).reshape(k // 32, 32, n)
    amax = np.abs(w).max(1)
    if fmt == "e4m3":
        byte = np.frexp(amax)[1] - 1 + 127 - 7
    else:
        mant, ex = np.frexp(amax / 6.0)
        byte = np.where(mant > 0.5, ex, ex - 1) + 127
    byte = np.clip(np.where(amax > 0, byte, 1), 1, 254)
    scaled = (w * np.exp2(127.0 - byte)[:, None, :]).reshape(k, n).astype(np.float32)
    by_word = np.ascontiguousarray(scaled.reshape(k // 512, 128, 4, n).transpose(0, 1, 3, 2))
    if fmt == "e4m3":
        words = by_word.astype(ml_dtypes.float8_e4m3fn).view(np.uint8)
    else:
        c = by_word.astype(ml_dtypes.float4_e2m1fn).view(np.uint8) & 0xF
        words = (c[..., 0::2] | (c[..., 1::2] << 4)).reshape(k // 512, 128, 2 * n)
    return np.ascontiguousarray(words), np.ascontiguousarray(byte.astype(np.uint8).reshape(k // 512, 16, n))


def unpack_weight(words, scales, fmt):
    g, _, n = scales.shape
    words = np.ascontiguousarray(words).reshape(g, 128, n, -1)
    if fmt == "e4m3":
        vals = words.view(ml_dtypes.float8_e4m3fn).astype(np.float64)
    else:
        nib = np.empty((g, 128, n, 4), np.uint8)
        nib[..., 0::2] = words & 0xF
        nib[..., 1::2] = words >> 4
        vals = E2M1[nib]
    vals = vals * np.repeat(np.exp2(scales.astype(np.float64) - 127.0), 8, axis=1)[..., None]
    return vals.transpose(0, 1, 3, 2).reshape(g * 512, n)


D, T, I, Q, J, U, M = 512, 2048, 512, 128, 512, 1024, 2048


def setup_inputs():
    n = np.random.standard_normal
    idx = np.random.permutation(T)[:I]
    idx2 = np.random.permutation(U)[:J]
    idx3 = np.random.permutation(M)[:I]
    fd = mx_kscale(D)
    fj = mx_kscale(J)
    tiesp = pack_weight(n((J, T)) * 0.08 / fj[:, None], "e4m3")
    return {
        "query": (n((D, Q)) * 1.0 / np.sqrt(D) * fd[:, None]).astype(np.float32),
        "hubs": (n((D, U)) / fd[:, None]).astype(np.float32),
        "hf": (np.random.uniform(0.5, 2.0, (J, 1)) * fj[:, None]).astype(np.float32),
        "ties_words": tiesp[0],
        "ties_scales": tiesp[1],
        "old": (np.random.uniform(0.0, 2.0, (Q, M))).astype(np.float32),
        "fade": (np.random.uniform(0.3, 0.9, (Q, 1))).astype(np.float32),
        "offs": striped(idx),
        "offs2": striped(idx2),
        "offs3": striped(idx3),
    }


def reference(query, hubs, hf, ties_words, ties_scales, old, fade, offs, offs2, offs3):
    idx = unstriped(offs)
    idx2 = unstriped(offs2)
    idx3 = unstriped(offs3)
    tiesu = unpack_weight(ties_words, ties_scales, "e4m3")
    hubsidx2q = mxq(f64(hubs)[:, idx2], 0, "e4m3")
    queryq = mxq(f64(query), 0, "e4m3")
    hb = hubsidx2q.T @ queryq
    hp = np.maximum(hb, 0.0) * f64(hf)
    hpq = mxq(hp, 0, "e4m3")
    tiesidxg = tiesu[:, idx]
    s = hpq.T @ tiesidxg
    w = np.maximum(s, 0.0)
    ws = w * 2.0
    wf = np.zeros((Q, M))
    wf[:, idx3] = ws
    y = f64(old) * f64(fade) + wf
    return y

@@ -1,0 +1,164 @@
+from contextlib import ExitStack
+
+import concourse.mybir as mybir
+
+D, T, I, Q, J, U, M = 512, 2048, 512, 128, 512, 1024, 2048
+FLOPS = 2 * D * J * Q + 2 * J * Q * I
+
+F32 = mybir.dt.float32
+BF16 = mybir.dt.bfloat16
+I32 = mybir.dt.int32
+U32 = mybir.dt.uint32
+U16 = mybir.dt.uint16
+U8 = mybir.dt.uint8
+FP8X4 = mybir.dt.float8_e4m3fn_x4
+ALU = mybir.AluOpType
+ACT = mybir.ActivationFunctionType
+
+P = 128
+PACK = 4
+STRIPE = 16
+LOAD_ORDER = (0, 1, 3, 2)
+VECTOR_SLOTS = (0, 320, 512, 0)
+PICKED_ROW = (0, 1, 1, 2)
+OUT_CHUNKS = (384, 640, 640, 384)
+
+
+def entries(offsets, first, last):
+    return offsets[:, first // STRIPE : last // STRIPE]
+
+
+def quantise(nc, codes, scales, values):
+    nc.vector.quantize_mx(out=codes.bitcast(FP8X4), scales=scales, in_=values)
+
+
+def tile_attend_relayed_counts_lean_kernel(tc, query, hubs, hf, ties_words, ties_scales, old, fade, offs, offs2, offs3, out):
+    nc = tc.nc
+    with ExitStack() as ctx:
+        sb = ctx.enter_context(tc.tile_pool(name="sb", bufs=1))
+        psum = ctx.enter_context(tc.psum_pool(name="psum", bufs=1))
+
+        token_list = sb.tile([P, I // STRIPE], U16, name="token_list")
+        hub_list = sb.tile([P, J // STRIPE], U16, name="hub_list")
+        column_list = sb.tile([P, I // STRIPE], U16, name="column_list")
+        hub_rows = [sb.tile([P, U], F32, name=f"hub_rows{t}") for t in range(PACK)]
+        query_rows = sb.tile([P, PACK, Q], F32, name="query_rows")
+        pool_words = sb.tile([P, T], I32, name="pool_words")
+        pool_scales = sb.tile([P, T], U8, name="pool_scales")
+        hub_factor = sb.tile([P, PACK], F32, name="hub_factor")
+        old_sb = sb.tile([P, M], F32, name="old_sb")
+        fade_sb = sb.tile([P, 1], F32, name="fade_sb")
+        placed = sb.tile([P, M], F32, name="placed")
+
+        nc.vector.memset(pool_scales[:].bitcast(I32), 0)
+        nc.vector.memset(placed[:], 0.0)
+
+        hub_planes = hubs.rearrange("(p t) u -> p t u", t=PACK)
+        nc.sync.dma_start(hub_list[:], offs2)
+        nc.sync.dma_start(token_list[:], offs)
+        nc.sync.dma_start(hub_rows[0][:], hub_planes[:, 0, :])
+        for f in range(4):
+            nc.sync.dma_start(pool_scales[f:P:32, :].bitcast(I32), ties_scales[0, f:16:4, :].bitcast(I32))
+        nc.sync.dma_start(query_rows[:], query.rearrange("(p t) q -> p t q", t=PACK))
+        for t in LOAD_ORDER[1:]:
+            nc.sync.dma_start(hub_rows[t][:], hub_planes[:, t, :])
+        nc.sync.dma_start(pool_words[:], ties_words[0].rearrange("p n t -> p (n t)").bitcast(I32))
+        nc.sync.dma_start(hub_factor[:], hf.rearrange("(p t) o -> p (t o)", t=PACK))
+        nc.sync.dma_start(column_list[:], offs3)
+        nc.sync.dma_start(old_sb[:], old)
+        nc.sync.dma_start(fade_sb[:], fade)
+
+        picked = sb.tile([P, 3, J], BF16, name="picked", align_bytes=64)
+        hub_in = sb.tile([P, PACK, P, PACK], BF16, name="hub_in", tag="hub_in", align_bytes=64)
+        hub_codes = [sb.tile([P, J // 2], U32, name=f"hub_codes{u}", align_bytes=64) for u in range(2)]
+        hub_scales = [sb.tile([P, J // 2], U8, name=f"hub_scales{u}", align_bytes=64) for u in range(2)]
+        query_in = sb.tile([P, Q, PACK], BF16, name="query_in", align_bytes=64)
+        query_codes = sb.tile([P, Q], U32, name="query_codes", align_bytes=64)
+        query_scales = sb.tile([P, Q], U8, name="query_scales", align_bytes=64)
+        tie_scales = sb.tile([P, I], U8, name="tie_scales", align_bytes=64)
+
+        def pick(t):
+            row = PICKED_ROW[t]
+            cut = VECTOR_SLOTS[t]
+            if cut > 0:
+                nc.vector.tensor_copy(picked[:, row, 0:cut], hub_rows[t][:].indirect(entries(hub_list, 0, cut)))
+            if cut < J:
+                nc.scalar.activation(picked[:, row, cut:J], hub_rows[t][:].indirect(entries(hub_list, cut, J)), ACT.Copy)
+
+        def weave(u):
+            nc.vector.tensor_copy(
+                hub_in[:].rearrange("p r s t -> p s t r")[:, :, 2 * u : 2 * u + 2, :],
+                picked[:, u : u + 2, :].rearrange("p e (s r) -> p s e r", r=PACK),
+            )
+
+        nc.vector.tensor_copy(tie_scales[:], pool_scales[:].indirect(token_list[:]))
+        nc.vector.tensor_copy(query_in[:], query_rows[:].rearrange("p t q -> p q t"))
+        pick(0)
+        pick(1)
+        quantise(nc, query_codes[:], query_scales[:], query_in[:].rearrange("p q t -> p (q t)"))
+        weave(0)
+        pick(3)
+        pick(2)
+        weave(1)
+
+        for u in range(2):
+            quantise(nc, hub_codes[u][:], hub_scales[u][:], hub_in[:, 2 * u : 2 * u + 2, :, :].rearrange("p r s t -> p (r s t)"))
+
+        hub_scores = psum.tile([P, PACK, Q], F32, name="hub_scores")
+        for r in range(PACK):
+            cols = slice(r % 2 * P, (r % 2 + 1) * P)
+            nc.tensor.matmul_mx(
+                out=hub_scores[:, r, :],
+                lhsT=hub_codes[r // 2][:, cols].bitcast(FP8X4),
+                lhsT_scale=hub_scales[r // 2][:, cols],
+                rhs=query_codes[:].bitcast(FP8X4),
+                rhs_scale=query_scales[:],
+                start=True,
+                stop=True,
+            )
+
+        half = I // 2
+        pool_view = pool_words[:].bitcast(U32)
+        first_words = sb.tile([P, half], U32, name="first_words", tag="hub_in", align_bytes=64)
+        nc.vector.tensor_copy(first_words[:], pool_view.indirect(entries(token_list, 0, half)))
+
+        relay_in = sb.tile([P, Q, PACK], BF16, name="relay_in", tag="relay_in", align_bytes=64)
+        relay_codes = sb.tile([P, Q], U32, name="relay_codes", align_bytes=64)
+        relay_scales = sb.tile([P, Q], U8, name="relay_scales", align_bytes=64)
+        nc.vector.scalar_tensor_tensor(
+            out=relay_in[:],
+            in0=hub_scores[:].rearrange("p r q -> p q r"),
+            scalar=0.0,
+            in1=hub_factor[:].unsqueeze(1).to_broadcast([P, Q, PACK]),
+            op0=ALU.max,
+            op1=ALU.mult,
+        )
+        quantise(nc, relay_codes[:], relay_scales[:], relay_in[:].rearrange("p q t -> p (q t)"))
+
+        second_words = sb.tile([P, half], U32, name="second_words", tag="relay_in", align_bytes=64)
+        nc.vector.tensor_copy(second_words[:], pool_view.indirect(entries(token_list, half, I)))
+
+        for h, words in enumerate((first_words, second_words)):
+            scores = psum.tile([P, half], F32, name=f"scores{h}")
+            nc.tensor.matmul_mx(
+                out=scores[:],
+                lhsT=relay_codes[:].bitcast(FP8X4),
+                lhsT_scale=relay_scales[:],
+                rhs=words[:].bitcast(FP8X4),
+                rhs_scale=tie_scales[:, h * half : (h + 1) * half],
+                start=True,
+                stop=True,
+            )
+            weights = sb.tile([P, half], F32, name=f"weights{h}")
+            nc.scalar.activation(weights[:], scores[:], ACT.Relu, scale=2.0)
+            nc.vector.tensor_copy(placed[:].indirect(entries(column_list, h * half, (h + 1) * half)), weights[:])
+
+        first = 0
+        for c, width in enumerate(OUT_CHUNKS):
+            cols = slice(first, first + width)
+            result = sb.tile([P, width], F32, name=f"result{c}")
+            nc.vector.scalar_tensor_tensor(
+                out=result[:], in0=old_sb[:, cols], scalar=fade_sb[:], in1=placed[:, cols], op0=ALU.mult, op1=ALU.add
+            )
+            nc.sync.dma_start(out[:, cols], result[:])
+            first = first + width

@@ -19,9 +19,8 @@ P = 128
 PACK = 4
 STRIPE = 16
 LOAD_ORDER = (0, 1, 3, 2)
-VECTOR_SLOTS = (0, 320, 512, 0)
-PICKED_ROW = (0, 1, 1, 2)
-OUT_CHUNKS = (384, 640, 640, 384)
+VECTOR_SLOTS = (0, 192, 288, 0)
+OUT_CHUNKS = (256, 576, 576, 512, 128)
 
 
 def entries(offsets, first, last):
@@ -41,12 +40,11 @@ def tile_attend_relayed_counts_lean_kernel(tc, query, hubs, hf, ties_words, ties
         token_list = sb.tile([P, I // STRIPE], U16, name="token_list")
         hub_list = sb.tile([P, J // STRIPE], U16, name="hub_list")
         column_list = sb.tile([P, I // STRIPE], U16, name="column_list")
-        hub_rows = [sb.tile([P, U], F32, name=f"hub_rows{t}") for t in range(PACK)]
+        hub_rows = [sb.tile([P, U], F32, name=f"hub_rows{t}", tag=f"hub_rows{t}", align_bytes=64) for t in range(PACK)]
         query_rows = sb.tile([P, PACK, Q], F32, name="query_rows")
         pool_words = sb.tile([P, T], I32, name="pool_words")
-        pool_scales = sb.tile([P, T], U8, name="pool_scales")
+        pool_scales = sb.tile([P, T], U8, name="pool_scales", tag="pool_scales")
         hub_factor = sb.tile([P, PACK], F32, name="hub_factor")
-        old_sb = sb.tile([P, M], F32, name="old_sb")
         fade_sb = sb.tile([P, 1], F32, name="fade_sb")
         placed = sb.tile([P, M], F32, name="placed")
 
@@ -57,49 +55,52 @@ def tile_attend_relayed_counts_lean_kernel(tc, query, hubs, hf, ties_words, ties
         nc.sync.dma_start(hub_list[:], offs2)
         nc.sync.dma_start(token_list[:], offs)
         nc.sync.dma_start(hub_rows[0][:], hub_planes[:, 0, :])
-        for f in range(4):
-            nc.sync.dma_start(pool_scales[f:P:32, :].bitcast(I32), ties_scales[0, f:16:4, :].bitcast(I32))
-        nc.sync.dma_start(query_rows[:], query.rearrange("(p t) q -> p t q", t=PACK))
+        nc.sync.dma_start(pool_scales[0:P:8, :].bitcast(I32), ties_scales[0].bitcast(I32))
         for t in LOAD_ORDER[1:]:
             nc.sync.dma_start(hub_rows[t][:], hub_planes[:, t, :])
+        nc.sync.dma_start(query_rows[:], query.rearrange("(p t) q -> p t q", t=PACK))
         nc.sync.dma_start(pool_words[:], ties_words[0].rearrange("p n t -> p (n t)").bitcast(I32))
         nc.sync.dma_start(hub_factor[:], hf.rearrange("(p t) o -> p (t o)", t=PACK))
         nc.sync.dma_start(column_list[:], offs3)
-        nc.sync.dma_start(old_sb[:], old)
         nc.sync.dma_start(fade_sb[:], fade)
 
-        picked = sb.tile([P, 3, J], BF16, name="picked", align_bytes=64)
+        picked = [sb.tile([P, 2, J], BF16, name=f"picked{u}", align_bytes=64) for u in range(2)]
         hub_in = sb.tile([P, PACK, P, PACK], BF16, name="hub_in", tag="hub_in", align_bytes=64)
         hub_codes = [sb.tile([P, J // 2], U32, name=f"hub_codes{u}", align_bytes=64) for u in range(2)]
         hub_scales = [sb.tile([P, J // 2], U8, name=f"hub_scales{u}", align_bytes=64) for u in range(2)]
-        query_in = sb.tile([P, Q, PACK], BF16, name="query_in", align_bytes=64)
         query_codes = sb.tile([P, Q], U32, name="query_codes", align_bytes=64)
         query_scales = sb.tile([P, Q], U8, name="query_scales", align_bytes=64)
         tie_scales = sb.tile([P, I], U8, name="tie_scales", align_bytes=64)
 
         def pick(t):
-            row = PICKED_ROW[t]
+            row = picked[t // 2][:, t % 2, :]
             cut = VECTOR_SLOTS[t]
             if cut > 0:
-                nc.vector.tensor_copy(picked[:, row, 0:cut], hub_rows[t][:].indirect(entries(hub_list, 0, cut)))
+                nc.vector.tensor_copy(row[:, 0:cut], hub_rows[t][:].indirect(entries(hub_list, 0, cut)))
             if cut < J:
-                nc.scalar.activation(picked[:, row, cut:J], hub_rows[t][:].indirect(entries(hub_list, cut, J)), ACT.Copy)
+                nc.scalar.activation(row[:, cut:J], hub_rows[t][:].indirect(entries(hub_list, cut, J)), ACT.Copy)
 
         def weave(u):
             nc.vector.tensor_copy(
                 hub_in[:].rearrange("p r s t -> p s t r")[:, :, 2 * u : 2 * u + 2, :],
-                picked[:, u : u + 2, :].rearrange("p e (s r) -> p s e r", r=PACK),
+                picked[u][:].rearrange("p e (s r) -> p s e r", r=PACK),
             )
 
-        nc.vector.tensor_copy(tie_scales[:], pool_scales[:].indirect(token_list[:]))
-        nc.vector.tensor_copy(query_in[:], query_rows[:].rearrange("p t q -> p q t"))
+        picked_scales = sb.tile([P, I], U8, name="picked_scales")
+        nc.vector.tensor_copy(picked_scales[:], pool_scales[:].indirect(token_list[:]))
+        for f in range(4):
+            nc.sync.dma_start(tie_scales[f:P:32, :].bitcast(I32), picked_scales[8 * f : P : 32, :].bitcast(I32))
+        old_sb = sb.tile([P, M], F32, name="old_sb", tag="pool_scales")
+        nc.sync.dma_start(old_sb[:], old)
         pick(0)
         pick(1)
-        quantise(nc, query_codes[:], query_scales[:], query_in[:].rearrange("p q t -> p (q t)"))
         weave(0)
         pick(3)
         pick(2)
         weave(1)
+        query_in = sb.tile([P, Q, PACK], BF16, name="query_in", tag=f"hub_rows{LOAD_ORDER[-1]}", align_bytes=64)
+        nc.scalar.copy(query_in[:], query_rows[:].rearrange("p t q -> p q t"))
+        quantise(nc, query_codes[:], query_scales[:], query_in[:].rearrange("p q t -> p (q t)"))
 
         for u in range(2):
             quantise(nc, hub_codes[u][:], hub_scales[u][:], hub_in[:, 2 * u : 2 * u + 2, :, :].rearrange("p r s t -> p (r s t)"))

@@ -49,6 +49,9 @@ def tile_attend_relayed_counts_lean_kernel(tc, query, hubs, hf, ties_words, ties
         placed = sb.tile([P, M], F32, name="placed")
 
         nc.vector.memset(pool_scales[:].bitcast(I32), 0)
+        warm = sb.tile([P, 2], F32, name="warm")
+        nc.gpsimd.memset(warm[:, 0:1], 0.0)
+        nc.scalar.activation(warm[:, 1:2], warm[:, 0:1], ACT.Copy)
         nc.vector.memset(placed[:], 0.0)
 
         hub_planes = hubs.rearrange("(p t) u -> p t u", t=PACK)

@@ -20,7 +20,7 @@ PACK = 4
 STRIPE = 16
 LOAD_ORDER = (0, 1, 3, 2)
 VECTOR_SLOTS = (0, 192, 288, 0)
-OUT_CHUNKS = (256, 576, 576, 512, 128)
+OUT_CHUNKS = (320, 512, 512, 512, 192)
 
 
 def entries(offsets, first, last):
@@ -48,17 +48,18 @@ def tile_attend_relayed_counts_lean_kernel(tc, query, hubs, hf, ties_words, ties
         fade_sb = sb.tile([P, 1], F32, name="fade_sb")
         placed = sb.tile([P, M], F32, name="placed")
 
-        nc.vector.memset(pool_scales[:].bitcast(I32), 0)
+        nc.vector.memset(pool_scales[:, 0 : T // 2].bitcast(I32), 0)
+        nc.gpsimd.memset(pool_scales[:, T // 2 : T].bitcast(I32), 0)
         warm = sb.tile([P, 2], F32, name="warm")
-        nc.gpsimd.memset(warm[:, 0:1], 0.0)
-        nc.scalar.activation(warm[:, 1:2], warm[:, 0:1], ACT.Copy)
+        nc.vector.memset(warm[:, 0:1], 0.0)
         nc.vector.memset(placed[:], 0.0)
 
         hub_planes = hubs.rearrange("(p t) u -> p t u", t=PACK)
+        nc.sync.dma_start(hub_rows[0][:], hub_planes[:, 0, :])
         nc.sync.dma_start(hub_list[:], offs2)
         nc.sync.dma_start(token_list[:], offs)
-        nc.sync.dma_start(hub_rows[0][:], hub_planes[:, 0, :])
         nc.sync.dma_start(pool_scales[0:P:8, :].bitcast(I32), ties_scales[0].bitcast(I32))
+        nc.scalar.activation(warm[:, 1:2], warm[:, 0:1], ACT.Copy)
         for t in LOAD_ORDER[1:]:
             nc.sync.dma_start(hub_rows[t][:], hub_planes[:, t, :])
         nc.sync.dma_start(query_rows[:], query.rearrange("(p t) q -> p t q", t=PACK))

@@ -18,9 +18,11 @@ ACT = mybir.ActivationFunctionType
 P = 128
 PACK = 4
 STRIPE = 16
-LOAD_ORDER = (0, 1, 3, 2)
-VECTOR_SLOTS = (0, 192, 288, 0)
-OUT_CHUNKS = (320, 512, 512, 512, 192)
+QUADRANT = 32
+BLOCK_ROWS = 8
+VECTOR_HUBS = (0, 192, 0, 288)
+FIRST_CHUNK, CHUNK = 320, 512
+OUT_CHUNKS = (FIRST_CHUNK, CHUNK, CHUNK, CHUNK, M - FIRST_CHUNK - 3 * CHUNK)
 
 
 def entries(offsets, first, last):
@@ -29,6 +31,18 @@ def entries(offsets, first, last):
 
 def quantise(nc, codes, scales, values):
     nc.vector.quantize_mx(out=codes.bitcast(FP8X4), scales=scales, in_=values)
+
+
+def product(nc, result, lhs_codes, lhs_scales, rhs_codes, rhs_scales):
+    nc.tensor.matmul_mx(
+        out=result,
+        lhsT=lhs_codes.bitcast(FP8X4),
+        lhsT_scale=lhs_scales,
+        rhs=rhs_codes.bitcast(FP8X4),
+        rhs_scale=rhs_scales,
+        start=True,
+        stop=True,
+    )
 
 
 def tile_attend_relayed_counts_lean_kernel(tc, query, hubs, hf, ties_words, ties_scales, old, fade, offs, offs2, offs3, out):
@@ -58,13 +72,13 @@ def tile_attend_relayed_counts_lean_kernel(tc, query, hubs, hf, ties_words, ties
         nc.sync.dma_start(hub_rows[0][:], hub_planes[:, 0, :])
         nc.sync.dma_start(hub_list[:], offs2)
         nc.sync.dma_start(token_list[:], offs)
-        nc.sync.dma_start(pool_scales[0:P:8, :].bitcast(I32), ties_scales[0].bitcast(I32))
+        nc.sync.dma_start(pool_scales[0:P:BLOCK_ROWS, :].bitcast(I32), ties_scales[0].bitcast(I32))
         nc.scalar.activation(warm[:, 1:2], warm[:, 0:1], ACT.Copy)
-        for t in LOAD_ORDER[1:]:
+        for t in range(1, PACK):
             nc.sync.dma_start(hub_rows[t][:], hub_planes[:, t, :])
         nc.sync.dma_start(query_rows[:], query.rearrange("(p t) q -> p t q", t=PACK))
         nc.sync.dma_start(pool_words[:], ties_words[0].rearrange("p n t -> p (n t)").bitcast(I32))
-        nc.sync.dma_start(hub_factor[:], hf.rearrange("(p t) o -> p (t o)", t=PACK))
+        nc.sync.dma_start(hub_factor[:], hf.rearrange("(p r) o -> p (r o)", r=PACK))
         nc.sync.dma_start(column_list[:], offs3)
         nc.sync.dma_start(fade_sb[:], fade)
 
@@ -76,51 +90,38 @@ def tile_attend_relayed_counts_lean_kernel(tc, query, hubs, hf, ties_words, ties
         query_scales = sb.tile([P, Q], U8, name="query_scales", align_bytes=64)
         tie_scales = sb.tile([P, I], U8, name="tie_scales", align_bytes=64)
 
-        def pick(t):
-            row = picked[t // 2][:, t % 2, :]
-            cut = VECTOR_SLOTS[t]
-            if cut > 0:
-                nc.vector.tensor_copy(row[:, 0:cut], hub_rows[t][:].indirect(entries(hub_list, 0, cut)))
-            if cut < J:
-                nc.scalar.activation(row[:, cut:J], hub_rows[t][:].indirect(entries(hub_list, cut, J)), ACT.Copy)
+        picked_scales = sb.tile([P, I], U8, name="picked_scales")
+        nc.vector.tensor_copy(picked_scales[:], pool_scales[:].indirect(token_list[:]))
+        for f in range(QUADRANT // BLOCK_ROWS):
+            nc.sync.dma_start(
+                tie_scales[f:P:QUADRANT, :].bitcast(I32), picked_scales[BLOCK_ROWS * f : P : QUADRANT, :].bitcast(I32)
+            )
+        old_sb = sb.tile([P, M], F32, name="old_sb", tag="pool_scales")
+        nc.sync.dma_start(old_sb[:], old)
 
-        def weave(u):
+        for u in range(2):
+            for e in range(2):
+                window = hub_rows[2 * u + e]
+                cut = VECTOR_HUBS[2 * u + e]
+                if cut > 0:
+                    nc.vector.tensor_copy(picked[u][:, e, 0:cut], window[:].indirect(entries(hub_list, 0, cut)))
+                nc.scalar.activation(picked[u][:, e, cut:J], window[:].indirect(entries(hub_list, cut, J)), ACT.Copy)
             nc.vector.tensor_copy(
                 hub_in[:].rearrange("p r s t -> p s t r")[:, :, 2 * u : 2 * u + 2, :],
                 picked[u][:].rearrange("p e (s r) -> p s e r", r=PACK),
             )
 
-        picked_scales = sb.tile([P, I], U8, name="picked_scales")
-        nc.vector.tensor_copy(picked_scales[:], pool_scales[:].indirect(token_list[:]))
-        for f in range(4):
-            nc.sync.dma_start(tie_scales[f:P:32, :].bitcast(I32), picked_scales[8 * f : P : 32, :].bitcast(I32))
-        old_sb = sb.tile([P, M], F32, name="old_sb", tag="pool_scales")
-        nc.sync.dma_start(old_sb[:], old)
-        pick(0)
-        pick(1)
-        weave(0)
-        pick(3)
-        pick(2)
-        weave(1)
-        query_in = sb.tile([P, Q, PACK], BF16, name="query_in", tag=f"hub_rows{LOAD_ORDER[-1]}", align_bytes=64)
+        query_in = sb.tile([P, Q, PACK], BF16, name="query_in", tag=f"hub_rows{PACK - 1}", align_bytes=64)
         nc.scalar.copy(query_in[:], query_rows[:].rearrange("p t q -> p q t"))
         quantise(nc, query_codes[:], query_scales[:], query_in[:].rearrange("p q t -> p (q t)"))
-
         for u in range(2):
-            quantise(nc, hub_codes[u][:], hub_scales[u][:], hub_in[:, 2 * u : 2 * u + 2, :, :].rearrange("p r s t -> p (r s t)"))
+            two_tiles = hub_in[:, 2 * u : 2 * u + 2, :, :].rearrange("p r s t -> p (r s t)")
+            quantise(nc, hub_codes[u][:], hub_scales[u][:], two_tiles)
 
         hub_scores = psum.tile([P, PACK, Q], F32, name="hub_scores")
         for r in range(PACK):
             cols = slice(r % 2 * P, (r % 2 + 1) * P)
-            nc.tensor.matmul_mx(
-                out=hub_scores[:, r, :],
-                lhsT=hub_codes[r // 2][:, cols].bitcast(FP8X4),
-                lhsT_scale=hub_scales[r // 2][:, cols],
-                rhs=query_codes[:].bitcast(FP8X4),
-                rhs_scale=query_scales[:],
-                start=True,
-                stop=True,
-            )
+            product(nc, hub_scores[:, r, :], hub_codes[r // 2][:, cols], hub_scales[r // 2][:, cols], query_codes[:], query_scales[:])
 
         half = I // 2
         pool_view = pool_words[:].bitcast(U32)
@@ -138,25 +139,28 @@ def tile_attend_relayed_counts_lean_kernel(tc, query, hubs, hf, ties_words, ties
             op0=ALU.max,
             op1=ALU.mult,
         )
-        quantise(nc, relay_codes[:], relay_scales[:], relay_in[:].rearrange("p q t -> p (q t)"))
+        quantise(nc, relay_codes[:], relay_scales[:], relay_in[:].rearrange("p q r -> p (q r)"))
 
         second_words = sb.tile([P, half], U32, name="second_words", tag="relay_in", align_bytes=64)
         nc.vector.tensor_copy(second_words[:], pool_view.indirect(entries(token_list, half, I)))
 
-        for h, words in enumerate((first_words, second_words)):
-            scores = psum.tile([P, half], F32, name=f"scores{h}")
-            nc.tensor.matmul_mx(
-                out=scores[:],
-                lhsT=relay_codes[:].bitcast(FP8X4),
-                lhsT_scale=relay_scales[:],
-                rhs=words[:].bitcast(FP8X4),
-                rhs_scale=tie_scales[:, h * half : (h + 1) * half],
-                start=True,
-                stop=True,
-            )
-            weights = sb.tile([P, half], F32, name=f"weights{h}")
-            nc.scalar.activation(weights[:], scores[:], ACT.Relu, scale=2.0)
-            nc.vector.tensor_copy(placed[:].indirect(entries(column_list, h * half, (h + 1) * half)), weights[:])
+        def slot_scores(name, words, first_slot):
+            count = words.shape[1]
+            scores = psum.tile([P, count], F32, name=name)
+            product(nc, scores[:], relay_codes[:], relay_scales[:], words, tie_scales[:, first_slot : first_slot + count])
+            return scores
+
+        quarter = I // 4
+        early_w = sb.tile([P, quarter], F32, name="early_w")
+        late_ws = sb.tile([P, I - quarter], F32, name="late_ws")
+        scores = slot_scores("scores_first", first_words[:, 0:quarter], 0)
+        nc.scalar.activation(early_w[:], scores[:], ACT.Relu)
+        scores = slot_scores("scores_second", first_words[:, quarter:half], quarter)
+        nc.scalar.activation(late_ws[:, 0:quarter], scores[:], ACT.Relu, scale=2.0)
+        scores = slot_scores("scores_last", second_words[:], half)
+        nc.scalar.activation(late_ws[:, quarter : I - quarter], scores[:], ACT.Relu, scale=2.0)
+        nc.vector.tensor_tensor(placed[:].indirect(entries(column_list, 0, quarter)), early_w[:], early_w[:], ALU.add)
+        nc.vector.tensor_copy(placed[:].indirect(entries(column_list, quarter, I)), late_ws[:])
 
         first = 0
         for c, width in enumerate(OUT_CHUNKS):

from contextlib import ExitStack

import concourse.mybir as mybir

D, T, I, Q, J, U, M = 512, 2048, 512, 128, 512, 1024, 2048
FLOPS = 2 * D * J * Q + 2 * J * Q * I

F32 = mybir.dt.float32
BF16 = mybir.dt.bfloat16
I32 = mybir.dt.int32
U32 = mybir.dt.uint32
U16 = mybir.dt.uint16
U8 = mybir.dt.uint8
FP8X4 = mybir.dt.float8_e4m3fn_x4
ALU = mybir.AluOpType
ACT = mybir.ActivationFunctionType

P = 128
PACK = 4
STRIPE = 16
QUADRANT = 32
BLOCK_ROWS = 8
VECTOR_HUBS = (0, 192, 0, 288)
FIRST_CHUNK, CHUNK = 320, 512
OUT_CHUNKS = (FIRST_CHUNK, CHUNK, CHUNK, CHUNK, M - FIRST_CHUNK - 3 * CHUNK)


def entries(offsets, first, last):
    return offsets[:, first // STRIPE : last // STRIPE]


def quantise(nc, codes, scales, values):
    nc.vector.quantize_mx(out=codes.bitcast(FP8X4), scales=scales, in_=values)


def product(nc, result, lhs_codes, lhs_scales, rhs_codes, rhs_scales):
    nc.tensor.matmul_mx(
        out=result,
        lhsT=lhs_codes.bitcast(FP8X4),
        lhsT_scale=lhs_scales,
        rhs=rhs_codes.bitcast(FP8X4),
        rhs_scale=rhs_scales,
        start=True,
        stop=True,
    )


def tile_attend_relayed_counts_lean_kernel(tc, query, hubs, hf, ties_words, ties_scales, old, fade, offs, offs2, offs3, out):
    nc = tc.nc
    with ExitStack() as ctx:
        sb = ctx.enter_context(tc.tile_pool(name="sb", bufs=1))
        psum = ctx.enter_context(tc.psum_pool(name="psum", bufs=1))

        token_list = sb.tile([P, I // STRIPE], U16, name="token_list")
        hub_list = sb.tile([P, J // STRIPE], U16, name="hub_list")
        column_list = sb.tile([P, I // STRIPE], U16, name="column_list")
        hub_rows = [sb.tile([P, U], F32, name=f"hub_rows{t}", tag=f"hub_rows{t}", align_bytes=64) for t in range(PACK)]
        query_rows = sb.tile([P, PACK, Q], F32, name="query_rows")
        pool_words = sb.tile([P, T], I32, name="pool_words")
        pool_scales = sb.tile([P, T], U8, name="pool_scales", tag="pool_scales")
        hub_factor = sb.tile([P, PACK], F32, name="hub_factor")
        fade_sb = sb.tile([P, 1], F32, name="fade_sb")
        placed = sb.tile([P, M], F32, name="placed")

        nc.vector.memset(pool_scales[:, 0 : T // 2].bitcast(I32), 0)
        nc.gpsimd.memset(pool_scales[:, T // 2 : T].bitcast(I32), 0)
        warm = sb.tile([P, 2], F32, name="warm")
        nc.vector.memset(warm[:, 0:1], 0.0)
        nc.vector.memset(placed[:], 0.0)

        hub_planes = hubs.rearrange("(p t) u -> p t u", t=PACK)
        nc.sync.dma_start(hub_rows[0][:], hub_planes[:, 0, :])
        nc.sync.dma_start(hub_list[:], offs2)
        nc.sync.dma_start(token_list[:], offs)
        nc.sync.dma_start(pool_scales[0:P:BLOCK_ROWS, :].bitcast(I32), ties_scales[0].bitcast(I32))
        nc.scalar.activation(warm[:, 1:2], warm[:, 0:1], ACT.Copy)
        for t in range(1, PACK):
            nc.sync.dma_start(hub_rows[t][:], hub_planes[:, t, :])
        nc.sync.dma_start(query_rows[:], query.rearrange("(p t) q -> p t q", t=PACK))
        nc.sync.dma_start(pool_words[:], ties_words[0].rearrange("p n t -> p (n t)").bitcast(I32))
        nc.sync.dma_start(hub_factor[:], hf.rearrange("(p r) o -> p (r o)", r=PACK))
        nc.sync.dma_start(column_list[:], offs3)
        nc.sync.dma_start(fade_sb[:], fade)

        picked = [sb.tile([P, 2, J], BF16, name=f"picked{u}", align_bytes=64) for u in range(2)]
        hub_in = sb.tile([P, PACK, P, PACK], BF16, name="hub_in", tag="hub_in", align_bytes=64)
        hub_codes = [sb.tile([P, J // 2], U32, name=f"hub_codes{u}", align_bytes=64) for u in range(2)]
        hub_scales = [sb.tile([P, J // 2], U8, name=f"hub_scales{u}", align_bytes=64) for u in range(2)]
        query_codes = sb.tile([P, Q], U32, name="query_codes", align_bytes=64)
        query_scales = sb.tile([P, Q], U8, name="query_scales", align_bytes=64)
        tie_scales = sb.tile([P, I], U8, name="tie_scales", align_bytes=64)

        picked_scales = sb.tile([P, I], U8, name="picked_scales")
        nc.vector.tensor_copy(picked_scales[:], pool_scales[:].indirect(token_list[:]))
        for f in range(QUADRANT // BLOCK_ROWS):
            nc.sync.dma_start(
                tie_scales[f:P:QUADRANT, :].bitcast(I32), picked_scales[BLOCK_ROWS * f : P : QUADRANT, :].bitcast(I32)
            )
        old_sb = sb.tile([P, M], F32, name="old_sb", tag="pool_scales")
        nc.sync.dma_start(old_sb[:], old)

        for u in range(2):
            for e in range(2):
                window = hub_rows[2 * u + e]
                cut = VECTOR_HUBS[2 * u + e]
                if cut > 0:
                    nc.vector.tensor_copy(picked[u][:, e, 0:cut], window[:].indirect(entries(hub_list, 0, cut)))
                nc.scalar.activation(picked[u][:, e, cut:J], window[:].indirect(entries(hub_list, cut, J)), ACT.Copy)
            nc.vector.tensor_copy(
                hub_in[:].rearrange("p r s t -> p s t r")[:, :, 2 * u : 2 * u + 2, :],
                picked[u][:].rearrange("p e (s r) -> p s e r", r=PACK),
            )

        query_in = sb.tile([P, Q, PACK], BF16, name="query_in", tag=f"hub_rows{PACK - 1}", align_bytes=64)
        nc.scalar.copy(query_in[:], query_rows[:].rearrange("p t q -> p q t"))
        quantise(nc, query_codes[:], query_scales[:], query_in[:].rearrange("p q t -> p (q t)"))
        for u in range(2):
            two_tiles = hub_in[:, 2 * u : 2 * u + 2, :, :].rearrange("p r s t -> p (r s t)")
            quantise(nc, hub_codes[u][:], hub_scales[u][:], two_tiles)

        hub_scores = psum.tile([P, PACK, Q], F32, name="hub_scores")
        for r in range(PACK):
            cols = slice(r % 2 * P, (r % 2 + 1) * P)
            product(nc, hub_scores[:, r, :], hub_codes[r // 2][:, cols], hub_scales[r // 2][:, cols], query_codes[:], query_scales[:])

        half = I // 2
        pool_view = pool_words[:].bitcast(U32)
        first_words = sb.tile([P, half], U32, name="first_words", tag="hub_in", align_bytes=64)
        nc.vector.tensor_copy(first_words[:], pool_view.indirect(entries(token_list, 0, half)))

        relay_in = sb.tile([P, Q, PACK], BF16, name="relay_in", tag="relay_in", align_bytes=64)
        relay_codes = sb.tile([P, Q], U32, name="relay_codes", align_bytes=64)
        relay_scales = sb.tile([P, Q], U8, name="relay_scales", align_bytes=64)
        nc.vector.scalar_tensor_tensor(
            out=relay_in[:],
            in0=hub_scores[:].rearrange("p r q -> p q r"),
            scalar=0.0,
            in1=hub_factor[:].unsqueeze(1).to_broadcast([P, Q, PACK]),
            op0=ALU.max,
            op1=ALU.mult,
        )
        quantise(nc, relay_codes[:], relay_scales[:], relay_in[:].rearrange("p q r -> p (q r)"))

        second_words = sb.tile([P, half], U32, name="second_words", tag="relay_in", align_bytes=64)
        nc.vector.tensor_copy(second_words[:], pool_view.indirect(entries(token_list, half, I)))

        def slot_scores(name, words, first_slot):
            count = words.shape[1]
            scores = psum.tile([P, count], F32, name=name)
            product(nc, scores[:], relay_codes[:], relay_scales[:], words, tie_scales[:, first_slot : first_slot + count])
            return scores

        quarter = I // 4
        early_w = sb.tile([P, quarter], F32, name="early_w")
        late_ws = sb.tile([P, I - quarter], F32, name="late_ws")
        scores = slot_scores("scores_first", first_words[:, 0:quarter], 0)
        nc.scalar.activation(early_w[:], scores[:], ACT.Relu)
        scores = slot_scores("scores_second", first_words[:, quarter:half], quarter)
        nc.scalar.activation(late_ws[:, 0:quarter], scores[:], ACT.Relu, scale=2.0)
        scores = slot_scores("scores_last", second_words[:], half)
        nc.scalar.activation(late_ws[:, quarter : I - quarter], scores[:], ACT.Relu, scale=2.0)
        nc.vector.tensor_tensor(placed[:].indirect(entries(column_list, 0, quarter)), early_w[:], early_w[:], ALU.add)
        nc.vector.tensor_copy(placed[:].indirect(entries(column_list, quarter, I)), late_ws[:])

        first = 0
        for c, width in enumerate(OUT_CHUNKS):
            cols = slice(first, first + width)
            result = sb.tile([P, width], F32, name=f"result{c}")
            nc.vector.scalar_tensor_tensor(
                out=result[:], in0=old_sb[:, cols], scalar=fade_sb[:], in1=placed[:, cols], op0=ALU.mult, op1=ALU.add
            )
            nc.sync.dma_start(out[:, cols], result[:])
            first = first + width
